import numpy as np
import ml_dtypes


def mxq(x, axis, fmt="e4m3"):
    dtype, down = {"e4m3": (ml_dtypes.float8_e4m3fn, 7), "e5m2": (ml_dtypes.float8_e5m2, 14)}[fmt]
    v = np.moveaxis(np.asarray(x, np.float32).astype(ml_dtypes.bfloat16).astype(np.float64), axis, -1)
    blocks = v.reshape(v.shape[:-1] + (-1, 32))
    amax = np.abs(blocks).max(-1, keepdims=True)
    byte = np.maximum(np.where(amax > 0, np.frexp(amax)[1] - 1 + 127, 0) - down, 1)
    scale = np.exp2(byte - 127.0)
    codes = (blocks / scale).astype(np.float32).astype(dtype).astype(np.float64)
    return np.moveaxis((codes * scale).reshape(v.shape), -1, axis)


WIDE = False


def mx_kscale(k):
    if not WIDE:
        return np.ones(k)
    levels = np.array([10, -10, 5, -5, 0])
    if k % 512:
        return np.exp2(np.random.permutation(np.resize(levels, k // 32))).repeat(32)
    a = np.empty((k // 512, 16))
    for p in range(k // 512):
        a[p, :8] = np.random.permutation(np.resize(levels, 8))
        for g in range(8):
            far = levels[np.abs(levels - a[p, g]) >= 10]
            a[p, g + 8] = far[np.random.randint(len(far))]
    return np.exp2(a.ravel()).repeat(32)


BF16 = ml_dtypes.bfloat16


def bf(x):
    return np.asarray(x, np.float32).astype(BF16)


def f64(x):
    return np.asarray(x).astype(np.float64)


E2M1 = np.array([0.0, 0.5, 1.0, 1.5, 2.0, 3.0, 4.0, 6.0, -0.0, -0.5, -1.0, -1.5, -2.0, -3.0, -4.0, -6.0])


def pack_weight(w, fmt):
    k, n = w.shape
    w = f64(bf(w)).reshape(k // 32, 32, n)
    amax = np.abs(w).max(1)
    if fmt == "e4m3":
        byte = np.frexp(amax)[1] - 1 + 127 - 7
    else:
        mant, ex = np.frexp(amax / 6.0)
        byte = np.where(mant > 0.5, ex, ex - 1) + 127
    byte = np.clip(np.where(amax > 0, byte, 1), 1, 254)
    scaled = (w * np.exp2(127.0 - byte)[:, None, :]).reshape(k, n).astype(np.float32)
    by_word = np.ascontiguousarray(scaled.reshape(k // 512, 128, 4, n).transpose(0, 1, 3, 2))
    if fmt == "e4m3":
        words = by_word.astype(ml_dtypes.float8_e4m3fn).view(np.uint8)
    else:
        c = by_word.astype(ml_dtypes.float4_e2m1fn).view(np.uint8) & 0xF
        words = c[..., 0::2] | (c[..., 1::2] << 4)
    return np.ascontiguousarray(words), np.ascontiguousarray(byte.astype(np.uint8).reshape(k // 512, 16, n))


def unpack_weight(words, scales, fmt):
    g, p, n, _ = words.shape
    if fmt == "e4m3":
        vals = np.ascontiguousarray(words).view(ml_dtypes.float8_e4m3fn).astype(np.float64)
    else:
        nib = np.empty((g, p, n, 4), np.uint8)
        nib[..., 0::2] = words & 0xF
        nib[..., 1::2] = words >> 4
        vals = E2M1[nib]
    vals = vals * np.repeat(np.exp2(scales.astype(np.float64) - 127.0), 8, axis=1)[..., None]
    return vals.transpose(0, 1, 3, 2).reshape(g * 512, n)
def pack4(w):
    words, scales = pack_weight(w, "e2m1")
    return words.reshape(words.shape[0], 128, -1), scales


def unpack4(words, scales):
    return unpack_weight(words.reshape(words.shape[0], 128, -1, 2), scales, "e2m1")


def planes(Y):
    n, m = Y.shape
    b = f64(bf(Y)).reshape(n // 32, 32, m)
    amax = np.abs(b).max(1)
    byte = np.clip(np.where(amax > 0, np.frexp(amax)[1] - 1 + 127 - 7, 1), 1, 254)
    codes = (b * np.exp2(127.0 - byte)[:, None, :]).reshape(n, m).astype(np.float32).astype(ml_dtypes.float8_e4m3fn).view(np.uint8)
    words = codes.reshape(n // 512, 128, 4, m).transpose(0, 1, 3, 2)
    return np.ascontiguousarray(words), np.ascontiguousarray(byte.astype(np.uint8).reshape(n // 512, 16, m))


U, K, N = 1024, 1536, 2048

def noise(*shape):
    return np.random.randn(*shape)

def setup_inputs():
    s = mx_kscale(K)
    density = np.random.uniform(0.4, 1.0, size=(U,))
    rated = np.random.rand(K, U) < density[None, :]
    spread = np.exp(0.7 * noise(U))
    ratings = np.where(rated, spread[None, :] * noise(K, U), 0.0)
    x_words, x_scales = pack_weight(ratings * s[:, None], "e4m3")
    size = np.exp(0.4 * noise(N))
    w = noise(K, N) / np.sqrt(K) * size[None, :]
    return {
        "x_words": x_words,
        "x_scales": x_scales,
        "w": bf(w / s[:, None]),
        "count_share": bf(rated.mean(axis=0)),
        "shrink": bf(np.random.uniform(0.05, 0.25, size=(N,))),
        "item_bias": bf(0.3 * noise(N)),
    }

def reference(x_words, x_scales, w, count_share, shrink, item_bias):
    X = unpack_weight(x_words, x_scales, "e4m3")
    W = mxq(f64(w), 0, "e4m3")
    A = X.T @ W
    count = f64(count_share)[:, None] + f64(shrink)[None, :]
    y = A / count + f64(item_bias)[None, :]
    Y = y
    words, scales = planes(Y)
    return y, words, scales

@@ -1,0 +1,288 @@
+from contextlib import ExitStack
+
+import concourse.mybir as mybir
+from concourse.masks import make_identity
+
+U, K, N = 1024, 1536, 2048
+FLOPS = 2 * U * K * N
+
+F32 = mybir.dt.float32
+BF16 = mybir.dt.bfloat16
+I32 = mybir.dt.int32
+U32 = mybir.dt.uint32
+U8 = mybir.dt.uint8
+FP8X4 = mybir.dt.float8_e4m3fn_x4
+ALU = mybir.AluOpType
+ACT = mybir.ActivationFunctionType
+
+P = 128
+PACK = 4
+KP = P * PACK
+PASSES = K // KP
+HALVES = U // KP
+NT = 512
+TILES = N // NT
+STEPS = TILES * HALVES
+HALF = NT // 2
+COUNT_FLOOR = 2.0**-40
+HEAD_V_COLS = 256
+
+
+def tile_shrunk_item_scores_g6_kernel(
+    tc, x_words, x_scales, w, count_share, shrink, item_bias, out_0, out_1, out_2
+):
+    nc = tc.nc
+    with ExitStack() as ctx:
+        keep = ctx.enter_context(tc.tile_pool(name="keep", bufs=1))
+        ring = ctx.enter_context(tc.tile_pool(name="ring", bufs=1))
+        psum = ctx.enter_context(tc.psum_pool(name="psum", bufs=1))
+        ctx.enter_context(tc.manual_schedule())
+
+        count_raw = keep.tile([P, HALVES, PACK], BF16, name="count_raw")
+        shrink_raw = keep.tile([P, TILES, PACK], BF16, name="shrink_raw")
+        bias_raw = keep.tile([P, TILES, PACK], BF16, name="bias_raw")
+        nc.scalar.dma_start(out=count_raw[:], in_=count_share.rearrange("(h p t) -> p h t", p=P, t=PACK))
+        nc.scalar.dma_start(out=shrink_raw[:], in_=shrink.rearrange("(n p c) -> p n c", p=P, c=PACK))
+        nc.scalar.dma_start(out=bias_raw[:], in_=item_bias.rearrange("(n p c) -> p n c", p=P, c=PACK))
+
+        xs_raw = keep.tile([P, U], U8, name="xs_raw", align_bytes=64)
+        nc.vector.memset(xs_raw[:].bitcast(I32), 0)
+        ident = keep.tile([P, P], F32, name="ident")
+        make_identity(nc, ident[:])
+        for q in range(4):
+            nc.gpsimd.dma_start(
+                out=xs_raw[32 * q : 32 * q + 4 * PASSES, :].bitcast(I32),
+                in_=x_scales[:, 4 * q : 4 * q + 4, :].bitcast(I32),
+            )
+
+        x_flat = x_words.rearrange("g p u t -> p g (u t)")
+        x_raw, w_raw = {}, {}
+
+        def load_x(h):
+            x_raw[h] = keep.tile([P, PASSES, KP], I32, name="x_raw%d" % h)
+            nc.sync.dma_start(out=x_raw[h][:], in_=x_flat[:, :, h * KP * PACK : (h + 1) * KP * PACK].bitcast(I32))
+
+        def load_w(n, g):
+            w_raw[n, g] = keep.tile([P, PACK, NT], BF16, name="w_raw%d_%d" % (n, g))
+            nc.sync.dma_start(
+                out=w_raw[n, g][:],
+                in_=w[g * KP : (g + 1) * KP, n * NT : (n + 1) * NT].rearrange("(p t) c -> p t c", t=PACK),
+            )
+
+        load_x(0)
+        for g in range(PASSES):
+            load_w(0, g)
+        load_x(1)
+        for n in range(1, TILES):
+            for g in range(PASSES):
+                load_w(n, g)
+
+        ncount = HALVES * PACK
+        nitem = TILES * PACK
+        positives = keep.tile([P, ncount + nitem], F32, name="positives")
+        logs = keep.tile([P, ncount + nitem], F32, name="logs")
+        inv_count = keep.tile([P, ncount], F32, name="inv_count")
+        bias32 = keep.tile([P, nitem], F32, name="bias32")
+        x_scale = keep.tile([P, U], U8, name="x_scale", align_bytes=64)
+        y_scale = keep.tile([P, N], U8, name="y_scale", align_bytes=64)
+        x_codes, w_grouped, w_codes, w_scale = {}, {}, {}, {}
+        log_bank, bias_bank, acc, share, y32, y16, y_codes = {}, {}, {}, {}, {}, {}, {}
+
+        def sort_x_codes(h):
+            x_codes[h] = keep.tile([P, PACK, PASSES, P], U32, name="x_codes%d" % h, align_bytes=64)
+            nc.vector.tensor_copy(
+                out=x_codes[h][:].bitcast(I32).rearrange("p t g (b i) -> p g b t i", i=4),
+                in_=x_raw[h][:].rearrange("p g (b i t) -> p g b t i", i=4, t=PACK),
+            )
+
+        def sort_x_scales():
+            nc.vector.tensor_copy(
+                out=x_scale[:].rearrange("p (h t b i) -> p h b t i", h=HALVES, t=PACK, i=16),
+                in_=xs_raw[:].rearrange("p (h b i t) -> p h b t i", h=HALVES, t=PACK, i=16),
+            )
+
+        def interleave(copy, dst, src, lo, hi):
+            copy(
+                out=dst[:, lo * PACK : hi * PACK].rearrange("p (c i t) -> p c t i", i=4, t=PACK),
+                in_=src[:, :, lo:hi].rearrange("p t (c i) -> p c t i", i=4),
+            )
+
+        def group_w(copy, n, g, lo, hi):
+            if (n, g) not in w_grouped:
+                w_grouped[n, g] = ring.tile([P, NT * PACK], BF16, name="w_grouped", bufs=4, align_bytes=64)
+            interleave(copy, w_grouped[n, g], w_raw[n, g], lo, hi)
+
+        def quantize_w(n, g):
+            w_codes[n, g] = keep.tile([P, NT], U32, name="w_codes%d_%d" % (n, g), align_bytes=64)
+            w_scale[n, g] = keep.tile([P, NT], U8, name="w_scale%d_%d" % (n, g), align_bytes=64)
+            nc.vector.quantize_mx(out=w_codes[n, g][:].bitcast(FP8X4), scales=w_scale[n, g][:], in_=w_grouped[n, g][:])
+
+        def spread(bank, cols, first):
+            by_slot = bank[:].rearrange("q (p c) -> q c p", c=PACK)
+            for c in range(PACK):
+                col = first + c
+                nc.tensor.transpose(by_slot[:, c, :], cols[:, col : col + 1].to_broadcast([P, P]), ident[:])
+
+        def spread_items(n):
+            log_bank[n] = psum.tile([P, NT], F32, name="log_bank", bufs=2)
+            spread(log_bank[n], logs, ncount + n * PACK)
+            bias_bank[n] = psum.tile([P, NT], F32, name="bias_bank", bufs=2)
+            spread(bias_bank[n], bias32, n * PACK)
+
+        def mx_pass(i, t, g):
+            n, h = divmod(i, HALVES)
+            if g == 0:
+                acc[i, t] = psum.tile([P, NT], F32, name="acc", bufs=4)
+            lo = h * KP + t * P
+            nc.tensor.matmul_mx(
+                out=acc[i, t][:],
+                lhsT=x_codes[h][:, t, g, :].bitcast(FP8X4),
+                lhsT_scale=x_scale[4 * g : P, lo : lo + P],
+                rhs=w_codes[n, g][:].bitcast(FP8X4),
+                rhs_scale=w_scale[n, g][:],
+                start=(g == 0),
+                stop=(g == PASSES - 1),
+            )
+
+        def product(i, t):
+            if i < STEPS:
+                for g in range(PASSES):
+                    mx_pass(i, t, g)
+
+        def sigmoid(i, t):
+            n, h = divmod(i, HALVES)
+            col = h * PACK + t
+            share[i, t] = ring.tile([P, NT], F32, name="share", bufs=8)
+            nc.scalar.activation(
+                out=share[i, t][:], in_=log_bank[n][:], func=ACT.Sigmoid, bias=logs[:, col : col + 1], scale=-1.0
+            )
+
+        def divide(i, t):
+            h = i % HALVES
+            col = h * PACK + t
+            if t == 0:
+                y32[i] = keep.tile([P, PACK, NT], F32, name="y32_%d" % i)
+            nc.vector.scalar_tensor_tensor(
+                out=y32[i][:, t, :], in0=acc[i, t][:], scalar=inv_count[:, col : col + 1], in1=share[i, t][:],
+                op0=ALU.mult, op1=ALU.mult,
+            )
+
+        def add_bias(i, lo, hi):
+            n = i // HALVES
+            nc.vector.tensor_tensor(
+                out=y32[i][:, :, lo:hi], in0=y32[i][:, :, lo:hi],
+                in1=bias_bank[n][:, lo:hi].unsqueeze(1).to_broadcast([P, PACK, hi - lo]), op=ALU.add,
+            )
+
+        def store_y(i, lo, hi):
+            n, h = divmod(i, HALVES)
+            rows = out_0[h * KP : (h + 1) * KP, n * NT + lo : n * NT + hi].rearrange("(p t) m -> p t m", t=PACK)
+            nc.sync.dma_start(out=rows, in_=y32[i][:, :, lo:hi])
+
+        def group_y(copy, i, lo, hi):
+            if i not in y16:
+                y16[i] = ring.tile([P, NT * PACK], BF16, name="y16", bufs=3, align_bytes=64)
+            interleave(copy, y16[i], y32[i], lo, hi)
+
+        def quantize_y(i, lo, hi):
+            n, h = divmod(i, HALVES)
+            if i not in y_codes:
+                y_codes[i] = keep.tile([P, NT], U32, name="y_codes%d" % i, align_bytes=64)
+            nc.vector.quantize_mx(
+                out=y_codes[i][:, lo:hi].bitcast(FP8X4),
+                scales=y_scale[4 * h : P, n * NT + lo : n * NT + hi],
+                in_=y16[i][:, lo * PACK : hi * PACK],
+            )
+
+        def store_codes(i):
+            n, h = divmod(i, HALVES)
+            dst = out_1[h].rearrange("p m t -> p (m t)")[:, n * NT * PACK : (n + 1) * NT * PACK]
+            nc.sync.dma_start(out=dst.bitcast(I32), in_=y_codes[i][:].bitcast(I32))
+
+        on_vector, on_scalar = nc.vector.tensor_copy, nc.scalar.copy
+
+        nc.vector.tensor_scalar(
+            out=positives[:, :ncount], in0=count_raw[:].rearrange("p h t -> p (h t)"),
+            scalar1=COUNT_FLOOR, scalar2=None, op0=ALU.max,
+        )
+        nc.vector.tensor_copy(out=positives[:, ncount:], in_=shrink_raw[:].rearrange("p n c -> p (n c)"))
+        nc.vector.tensor_copy(out=bias32[:], in_=bias_raw[:].rearrange("p n c -> p (n c)"))
+        nc.vector.reciprocal(out=inv_count[:], in_=positives[:, :ncount])
+        nc.scalar.activation(out=logs[:], in_=positives[:], func=ACT.Ln)
+        spread_items(0)
+        sigmoid(0, 0)
+        sort_x_codes(0)
+        for g in range(PASSES):
+            group_w(on_vector, 0, g, 0, HEAD_V_COLS)
+            group_w(on_scalar, 0, g, HEAD_V_COLS, NT)
+            if g == 1:
+                quantize_w(0, 0)
+                sort_x_scales()
+        quantize_w(0, 1)
+        quantize_w(0, 2)
+        for g in range(PASSES):
+            for t in range(PACK):
+                mx_pass(0, t, g)
+        for t in range(1, PACK):
+            sigmoid(0, t)
+        sort_x_codes(1)
+
+        for i in range(STEPS):
+            n, h = divmod(i, HALVES)
+            more = n + 1 < TILES
+            if more:
+                group_w(on_scalar, n + 1, 2 * h, 0, NT)
+            divide(i, 0)
+            if h == 0:
+                product(i + 1, 0)
+            if i > 0:
+                add_bias(i - 1, 0, HALF)
+            divide(i, 1)
+            if h == 0:
+                product(i + 1, 1)
+            if i > 0:
+                add_bias(i - 1, HALF, NT)
+                store_y(i - 1, 0, NT)
+            if h == 0 and more:
+                spread_items(n + 1)
+            if i + 1 < STEPS:
+                for t in range(PACK):
+                    sigmoid(i + 1, t)
+            if i > 0:
+                group_y(on_scalar, i - 1, 0, NT)
+            if h == 1 and more:
+                quantize_w(n + 1, 2)
+            if h == 1:
+                product(i + 1, 0)
+                product(i + 1, 1)
+            divide(i, 2)
+            product(i + 1, 2)
+            if h == 0 and more:
+                group_w(on_vector, n + 1, 1, 0, NT)
+            if i > 1:
+                quantize_y(i - 2, 0, NT)
+                store_codes(i - 2)
+            divide(i, 3)
+            product(i + 1, 3)
+            if h == 0 and more:
+                quantize_w(n + 1, 0)
+                quantize_w(n + 1, 1)
+
+        last = STEPS - 1
+        add_bias(last, 0, HALF)
+        store_y(last, 0, HALF)
+        group_y(on_scalar, last, 0, HALF)
+        add_bias(last, HALF, NT)
+        store_y(last, HALF, NT)
+        quantize_y(last - 1, 0, NT)
+        store_codes(last - 1)
+        group_y(on_vector, last, HALF, NT)
+        quantize_y(last, 0, HALF)
+        quantize_y(last, HALF, NT)
+        store_codes(last)
+        for q in range(4):
+            queue = nc.sync if q % 2 == 0 else nc.scalar
+            queue.dma_start(
+                out=out_2[:, 4 * q : 4 * q + 4, :].bitcast(I32),
+                in_=y_scale[32 * q : 32 * q + 4 * HALVES, :].bitcast(I32),
+            )

@@ -26,6 +26,7 @@ STEPS = TILES * HALVES
 HALF = NT // 2
 COUNT_FLOOR = 2.0**-40
 HEAD_V_COLS = 256
+TAIL_SPLIT = 352
 
 
 def tile_shrunk_item_scores_g6_kernel(
@@ -49,11 +50,6 @@ def tile_shrunk_item_scores_g6_kernel(
         nc.vector.memset(xs_raw[:].bitcast(I32), 0)
         ident = keep.tile([P, P], F32, name="ident")
         make_identity(nc, ident[:])
-        for q in range(4):
-            nc.gpsimd.dma_start(
-                out=xs_raw[32 * q : 32 * q + 4 * PASSES, :].bitcast(I32),
-                in_=x_scales[:, 4 * q : 4 * q + 4, :].bitcast(I32),
-            )
 
         x_flat = x_words.rearrange("g p u t -> p g (u t)")
         x_raw, w_raw = {}, {}
@@ -70,8 +66,14 @@ def tile_shrunk_item_scores_g6_kernel(
             )
 
         load_x(0)
-        for g in range(PASSES):
-            load_w(0, g)
+        load_w(0, 0)
+        for q in range(4):
+            nc.sync.dma_start(
+                out=xs_raw[32 * q : 32 * q + 4 * PASSES, :].bitcast(I32),
+                in_=x_scales[:, 4 * q : 4 * q + 4, :].bitcast(I32),
+            )
+        load_w(0, 1)
+        load_w(0, 2)
         load_x(1)
         for n in range(1, TILES):
             for g in range(PASSES):
@@ -107,9 +109,15 @@ def tile_shrunk_item_scores_g6_kernel(
                 in_=src[:, :, lo:hi].rearrange("p t (c i) -> p c t i", i=4),
             )
 
+        def on_gpsimd(out, in_):
+            nc.gpsimd.tensor_scalar(out=out, in0=in_, scalar1=1.0, scalar2=0.0, op0=ALU.mult, op1=ALU.add)
+
         def group_w(copy, n, g, lo, hi):
             if (n, g) not in w_grouped:
-                w_grouped[n, g] = ring.tile([P, NT * PACK], BF16, name="w_grouped", bufs=4, align_bytes=64)
+                if copy is on_gpsimd:
+                    w_grouped[n, g] = ring.tile([P, NT * PACK], BF16, name="w_grouped_one", bufs=1, align_bytes=64)
+                else:
+                    w_grouped[n, g] = ring.tile([P, NT * PACK], BF16, name="w_grouped", bufs=3, align_bytes=64)
             interleave(copy, w_grouped[n, g], w_raw[n, g], lo, hi)
 
         def quantize_w(n, g):
@@ -144,10 +152,6 @@ def tile_shrunk_item_scores_g6_kernel(
                 stop=(g == PASSES - 1),
             )
 
-        def product(i, t):
-            if i < STEPS:
-                for g in range(PASSES):
-                    mx_pass(i, t, g)
 
         def sigmoid(i, t):
             n, h = divmod(i, HALVES)
@@ -157,13 +161,14 @@ def tile_shrunk_item_scores_g6_kernel(
                 out=share[i, t][:], in_=log_bank[n][:], func=ACT.Sigmoid, bias=logs[:, col : col + 1], scale=-1.0
             )
 
-        def divide(i, t):
+        def divide(i, t, lo, hi):
             h = i % HALVES
             col = h * PACK + t
-            if t == 0:
+            if i not in y32:
                 y32[i] = keep.tile([P, PACK, NT], F32, name="y32_%d" % i)
             nc.vector.scalar_tensor_tensor(
-                out=y32[i][:, t, :], in0=acc[i, t][:], scalar=inv_count[:, col : col + 1], in1=share[i, t][:],
+                out=y32[i][:, t, lo:hi], in0=acc[i, t][:, lo:hi], scalar=inv_count[:, col : col + 1],
+                in1=share[i, t][:, lo:hi],
                 op0=ALU.mult, op1=ALU.mult,
             )
 
@@ -215,69 +220,75 @@ def tile_shrunk_item_scores_g6_kernel(
         for g in range(PASSES):
             group_w(on_vector, 0, g, 0, HEAD_V_COLS)
             group_w(on_scalar, 0, g, HEAD_V_COLS, NT)
-            if g == 1:
-                quantize_w(0, 0)
+            if g == 0:
                 sort_x_scales()
-        quantize_w(0, 1)
+            else:
+                quantize_w(0, g - 1)
         quantize_w(0, 2)
-        for g in range(PASSES):
-            for t in range(PACK):
-                mx_pass(0, t, g)
+        for t in range(PACK):
+            mx_pass(0, t, 0)
+        for t in range(PACK):
+            mx_pass(0, t, 1)
+            mx_pass(0, t, 2)
         for t in range(1, PACK):
             sigmoid(0, t)
         sort_x_codes(1)
 
+        last = STEPS - 1
         for i in range(STEPS):
             n, h = divmod(i, HALVES)
             more = n + 1 < TILES
-            if more:
-                group_w(on_scalar, n + 1, 2 * h, 0, NT)
-            divide(i, 0)
-            if h == 0:
-                product(i + 1, 0)
-            if i > 0:
-                add_bias(i - 1, 0, HALF)
-            divide(i, 1)
-            if h == 0:
-                product(i + 1, 1)
-            if i > 0:
-                add_bias(i - 1, HALF, NT)
-                store_y(i - 1, 0, NT)
-            if h == 0 and more:
-                spread_items(n + 1)
-            if i + 1 < STEPS:
-                for t in range(PACK):
-                    sigmoid(i + 1, t)
-            if i > 0:
-                group_y(on_scalar, i - 1, 0, NT)
-            if h == 1 and more:
-                quantize_w(n + 1, 2)
-            if h == 1:
-                product(i + 1, 0)
-                product(i + 1, 1)
-            divide(i, 2)
-            product(i + 1, 2)
-            if h == 0 and more:
-                group_w(on_vector, n + 1, 1, 0, NT)
             if i > 1:
                 quantize_y(i - 2, 0, NT)
                 store_codes(i - 2)
-            divide(i, 3)
-            product(i + 1, 3)
-            if h == 0 and more:
+            if h == 0 and i > 0:
+                quantize_w(n, 1)
+                quantize_w(n, 2)
+                for t in range(PACK):
+                    mx_pass(i, t, 1)
+                    mx_pass(i, t, 2)
+            if i == 1:
+                add_bias(0, 0, HALF)
+            if h == 1 and more:
                 quantize_w(n + 1, 0)
-                quantize_w(n + 1, 1)
+            if more:
+                group_w(on_gpsimd, n + 1, 2 * h, 0, NT)
+            if h == 1 and more:
+                group_w(on_scalar, n + 1, 1, 0, NT)
+            if h == 0:
+                for t in range(PACK):
+                    sigmoid(i + 1, t)
+            if i > 0:
+                for lo in (0, HALF):
+                    if (i, lo) != (1, 0):
+                        add_bias(i - 1, lo, lo + HALF)
+                    group_y(on_scalar, i - 1, lo, lo + HALF)
+                store_y(i - 1, 0, NT)
+            if h == 0 and more:
+                spread_items(n + 1)
+            if h == 1 and more:
+                for t in range(PACK):
+                    sigmoid(i + 1, t)
+            if i < last:
+                for t in range(PACK):
+                    divide(i, t, 0, NT)
+                    for g in range(PASSES if h == 0 else 1):
+                        mx_pass(i + 1, t, g)
 
-        last = STEPS - 1
+        for t in range(PACK):
+            divide(last, t, 0, HALF)
+        quantize_y(last - 1, 0, NT)
+        store_codes(last - 1)
         add_bias(last, 0, HALF)
         store_y(last, 0, HALF)
         group_y(on_scalar, last, 0, HALF)
+        for t in range(PACK):
+            divide(last, t, HALF, NT)
+        quantize_y(last, 0, HALF)
         add_bias(last, HALF, NT)
         store_y(last, HALF, NT)
-        quantize_y(last - 1, 0, NT)
-        store_codes(last - 1)
-        group_y(on_vector, last, HALF, NT)
-        quantize_y(last, 0, HALF)
+        group_y(on_scalar, last, HALF, TAIL_SPLIT)
+        group_y(on_vector, last, TAIL_SPLIT, NT)
         quantize_y(last, HALF, NT)
         store_codes(last)
         for q in range(4):

@@ -27,6 +27,7 @@ HALF = NT // 2
 COUNT_FLOOR = 2.0**-40
 HEAD_V_COLS = 256
 TAIL_SPLIT = 352
+GP_COLS = 128
 
 
 def tile_shrunk_item_scores_g6_kernel(
@@ -114,11 +115,17 @@ def tile_shrunk_item_scores_g6_kernel(
 
         def group_w(copy, n, g, lo, hi):
             if (n, g) not in w_grouped:
-                if copy is on_gpsimd:
+                if n > 0 and g != 1:
                     w_grouped[n, g] = ring.tile([P, NT * PACK], BF16, name="w_grouped_one", bufs=1, align_bytes=64)
                 else:
                     w_grouped[n, g] = ring.tile([P, NT * PACK], BF16, name="w_grouped", bufs=3, align_bytes=64)
-            interleave(copy, w_grouped[n, g], w_raw[n, g], lo, hi)
+            if copy is on_gpsimd:
+                copy(
+                    out=w_grouped[n, g][:, lo * PACK : hi * PACK].rearrange("p (c t) -> p c t", t=PACK),
+                    in_=w_raw[n, g][:, :, lo:hi].rearrange("p t c -> p c t"),
+                )
+            else:
+                interleave(copy, w_grouped[n, g], w_raw[n, g], lo, hi)
 
         def quantize_w(n, g):
             w_codes[n, g] = keep.tile([P, NT], U32, name="w_codes%d_%d" % (n, g), align_bytes=64)
@@ -253,8 +260,10 @@ def tile_shrunk_item_scores_g6_kernel(
                 quantize_w(n + 1, 0)
             if more:
                 group_w(on_gpsimd, n + 1, 2 * h, 0, NT)
+                if n > 0:
+                    group_w(on_gpsimd, n + 1, 1, h * GP_COLS, (h + 1) * GP_COLS)
             if h == 1 and more:
-                group_w(on_scalar, n + 1, 1, 0, NT)
+                group_w(on_scalar, n + 1, 1, 2 * GP_COLS if n > 0 else 0, NT)
             if h == 0:
                 for t in range(PACK):
                     sigmoid(i + 1, t)

@@ -26,8 +26,7 @@ STEPS = TILES * HALVES
 HALF = NT // 2
 COUNT_FLOOR = 2.0**-40
 HEAD_V_COLS = 256
-TAIL_SPLIT = 352
-GP_COLS = 128
+QUARTER = NT // 4
 
 
 def tile_shrunk_item_scores_g6_kernel(
@@ -66,8 +65,8 @@ def tile_shrunk_item_scores_g6_kernel(
                 in_=w[g * KP : (g + 1) * KP, n * NT : (n + 1) * NT].rearrange("(p t) c -> p t c", t=PACK),
             )
 
-        load_x(0)
         load_w(0, 0)
+        load_x(0)
         for q in range(4):
             nc.sync.dma_start(
                 out=xs_raw[32 * q : 32 * q + 4 * PASSES, :].bitcast(I32),
@@ -88,7 +87,7 @@ def tile_shrunk_item_scores_g6_kernel(
         bias32 = keep.tile([P, nitem], F32, name="bias32")
         x_scale = keep.tile([P, U], U8, name="x_scale", align_bytes=64)
         y_scale = keep.tile([P, N], U8, name="y_scale", align_bytes=64)
-        x_codes, w_grouped, w_codes, w_scale = {}, {}, {}, {}
+        x_codes, w_grouped, w_codes, w_scale, bias_rows = {}, {}, {}, {}, {}
         log_bank, bias_bank, acc, share, y32, y16, y_codes = {}, {}, {}, {}, {}, {}, {}
 
         def sort_x_codes(h):
@@ -174,8 +173,8 @@ def tile_shrunk_item_scores_g6_kernel(
             if i not in y32:
                 y32[i] = keep.tile([P, PACK, NT], F32, name="y32_%d" % i)
             nc.vector.scalar_tensor_tensor(
-                out=y32[i][:, t, lo:hi], in0=acc[i, t][:, lo:hi], scalar=inv_count[:, col : col + 1],
-                in1=share[i, t][:, lo:hi],
+                out=y32[i][:, t, lo:hi], in0=share[i, t][:, lo:hi], scalar=inv_count[:, col : col + 1],
+                in1=acc[i, t][:, lo:hi],
                 op0=ALU.mult, op1=ALU.mult,
             )
 
@@ -185,6 +184,24 @@ def tile_shrunk_item_scores_g6_kernel(
                 out=y32[i][:, :, lo:hi], in0=y32[i][:, :, lo:hi],
                 in1=bias_bank[n][:, lo:hi].unsqueeze(1).to_broadcast([P, PACK, hi - lo]), op=ALU.add,
             )
+
+        def copy_bias(copy, n):
+            bias_rows[n] = keep.tile([P, HALF], F32, name="bias_rows%d" % n)
+            copy(out=bias_rows[n][:], in_=bias_bank[n][:, HALF:])
+
+        def add_bias_gpsimd(i):
+            nc.gpsimd.tensor_tensor(
+                out=y32[i][:, :, HALF:], in0=y32[i][:, :, HALF:],
+                in1=bias_rows[i // HALVES][:].unsqueeze(1).to_broadcast([P, PACK, HALF]), op=ALU.add,
+            )
+
+        def store_scales(lo, hi):
+            for q in range(4):
+                queue = nc.sync if q % 2 == 0 or lo == 0 else nc.scalar
+                queue.dma_start(
+                    out=out_2[:, 4 * q : 4 * q + 4, lo:hi].bitcast(I32),
+                    in_=y_scale[32 * q : 32 * q + 4 * HALVES, lo:hi].bitcast(I32),
+                )
 
         def store_y(i, lo, hi):
             n, h = divmod(i, HALVES)
@@ -206,10 +223,10 @@ def tile_shrunk_item_scores_g6_kernel(
                 in_=y16[i][:, lo * PACK : hi * PACK],
             )
 
-        def store_codes(i):
+        def store_codes(i, lo, hi):
             n, h = divmod(i, HALVES)
-            dst = out_1[h].rearrange("p m t -> p (m t)")[:, n * NT * PACK : (n + 1) * NT * PACK]
-            nc.sync.dma_start(out=dst.bitcast(I32), in_=y_codes[i][:].bitcast(I32))
+            dst = out_1[h].rearrange("p m t -> p (m t)")[:, (n * NT + lo) * PACK : (n * NT + hi) * PACK]
+            nc.sync.dma_start(out=dst.bitcast(I32), in_=y_codes[i][:, lo:hi].bitcast(I32))
 
         on_vector, on_scalar = nc.vector.tensor_copy, nc.scalar.copy
 
@@ -223,14 +240,14 @@ def tile_shrunk_item_scores_g6_kernel(
         nc.scalar.activation(out=logs[:], in_=positives[:], func=ACT.Ln)
         spread_items(0)
         sigmoid(0, 0)
+        group_w(on_vector, 0, 0, 0, NT)
         sort_x_codes(0)
-        for g in range(PASSES):
+        quantize_w(0, 0)
+        for g in (1, 2):
             group_w(on_vector, 0, g, 0, HEAD_V_COLS)
             group_w(on_scalar, 0, g, HEAD_V_COLS, NT)
-            if g == 0:
-                sort_x_scales()
-            else:
-                quantize_w(0, g - 1)
+        sort_x_scales()
+        quantize_w(0, 1)
         quantize_w(0, 2)
         for t in range(PACK):
             mx_pass(0, t, 0)
@@ -242,12 +259,14 @@ def tile_shrunk_item_scores_g6_kernel(
         sort_x_codes(1)
 
         last = STEPS - 1
-        for i in range(STEPS):
+        for i in range(last):
             n, h = divmod(i, HALVES)
             more = n + 1 < TILES
             if i > 1:
                 quantize_y(i - 2, 0, NT)
-                store_codes(i - 2)
+                store_codes(i - 2, 0, NT)
+            if i - 2 == STEPS // 2 - 1:
+                store_scales(0, N // 2)
             if h == 0 and i > 0:
                 quantize_w(n, 1)
                 quantize_w(n, 2)
@@ -260,16 +279,20 @@ def tile_shrunk_item_scores_g6_kernel(
                 quantize_w(n + 1, 0)
             if more:
                 group_w(on_gpsimd, n + 1, 2 * h, 0, NT)
-                if n > 0:
-                    group_w(on_gpsimd, n + 1, 1, h * GP_COLS, (h + 1) * GP_COLS)
             if h == 1 and more:
-                group_w(on_scalar, n + 1, 1, 2 * GP_COLS if n > 0 else 0, NT)
+                group_w(on_scalar, n + 1, 1, 0, NT)
+            if i == last - 1:
+                copy_bias(on_vector, n - 1)
             if h == 0:
                 for t in range(PACK):
                     sigmoid(i + 1, t)
+            if i == last - 1:
+                copy_bias(on_scalar, n)
             if i > 0:
                 for lo in (0, HALF):
-                    if (i, lo) != (1, 0):
+                    if lo == HALF and not more:
+                        add_bias_gpsimd(i - 1)
+                    elif (i, lo) != (1, 0):
                         add_bias(i - 1, lo, lo + HALF)
                     group_y(on_scalar, i - 1, lo, lo + HALF)
                 store_y(i - 1, 0, NT)
@@ -278,31 +301,39 @@ def tile_shrunk_item_scores_g6_kernel(
             if h == 1 and more:
                 for t in range(PACK):
                     sigmoid(i + 1, t)
-            if i < last:
-                for t in range(PACK):
-                    divide(i, t, 0, NT)
-                    for g in range(PASSES if h == 0 else 1):
-                        mx_pass(i + 1, t, g)
+            for t in range(PACK):
+                divide(i, t, 0, NT)
+                for g in range(PASSES if h == 0 else 1):
+                    mx_pass(i + 1, t, g)
 
-        for t in range(PACK):
+        cut = HALF + QUARTER
+        divide(last, 0, 0, HALF)
+        add_bias_gpsimd(last - 1)
+        add_bias(last - 1, 0, HALF)
+        for lo in (0, HALF):
+            store_y(last - 1, lo, lo + HALF)
+            group_y(on_scalar, last - 1, lo, lo + HALF)
+        for t in range(1, PACK):
             divide(last, t, 0, HALF)
-        quantize_y(last - 1, 0, NT)
-        store_codes(last - 1)
+        divide(last, 0, HALF, NT)
         add_bias(last, 0, HALF)
         store_y(last, 0, HALF)
         group_y(on_scalar, last, 0, HALF)
-        for t in range(PACK):
+        quantize_y(last - 2, 0, NT)
+        store_codes(last - 2, 0, NT)
+        for t in range(1, PACK):
             divide(last, t, HALF, NT)
+        quantize_y(last - 1, 0, NT)
+        store_codes(last - 1, 0, NT)
+        add_bias(last, HALF, cut)
+        store_y(last, HALF, cut)
+        group_y(on_scalar, last, HALF, cut)
+        add_bias(last, cut, NT)
+        store_y(last, cut, NT)
         quantize_y(last, 0, HALF)
-        add_bias(last, HALF, NT)
-        store_y(last, HALF, NT)
-        group_y(on_scalar, last, HALF, TAIL_SPLIT)
-        group_y(on_vector, last, TAIL_SPLIT, NT)
-        quantize_y(last, HALF, NT)
-        store_codes(last)
-        for q in range(4):
-            queue = nc.sync if q % 2 == 0 else nc.scalar
-            queue.dma_start(
-                out=out_2[:, 4 * q : 4 * q + 4, :].bitcast(I32),
-                in_=y_scale[32 * q : 32 * q + 4 * HALVES, :].bitcast(I32),
-            )
+        store_codes(last, 0, HALF)
+        group_y(on_vector, last, cut, NT)
+        quantize_y(last, HALF, cut)
+        quantize_y(last, cut, NT)
+        store_codes(last, HALF, NT)
+        store_scales(N // 2, N)

from contextlib import ExitStack

import concourse.mybir as mybir
from concourse.masks import make_identity

U, K, N = 1024, 1536, 2048
FLOPS = 2 * U * K * N

F32 = mybir.dt.float32
BF16 = mybir.dt.bfloat16
I32 = mybir.dt.int32
U32 = mybir.dt.uint32
U8 = mybir.dt.uint8
FP8X4 = mybir.dt.float8_e4m3fn_x4
ALU = mybir.AluOpType
ACT = mybir.ActivationFunctionType

P = 128
PACK = 4
KP = P * PACK
PASSES = K // KP
HALVES = U // KP
NT = 512
TILES = N // NT
STEPS = TILES * HALVES
HALF = NT // 2
COUNT_FLOOR = 2.0**-40
HEAD_V_COLS = 256
QUARTER = NT // 4


def tile_shrunk_item_scores_g6_kernel(
    tc, x_words, x_scales, w, count_share, shrink, item_bias, out_0, out_1, out_2
):
    nc = tc.nc
    with ExitStack() as ctx:
        keep = ctx.enter_context(tc.tile_pool(name="keep", bufs=1))
        ring = ctx.enter_context(tc.tile_pool(name="ring", bufs=1))
        psum = ctx.enter_context(tc.psum_pool(name="psum", bufs=1))
        ctx.enter_context(tc.manual_schedule())

        count_raw = keep.tile([P, HALVES, PACK], BF16, name="count_raw")
        shrink_raw = keep.tile([P, TILES, PACK], BF16, name="shrink_raw")
        bias_raw = keep.tile([P, TILES, PACK], BF16, name="bias_raw")
        nc.scalar.dma_start(out=count_raw[:], in_=count_share.rearrange("(h p t) -> p h t", p=P, t=PACK))
        nc.scalar.dma_start(out=shrink_raw[:], in_=shrink.rearrange("(n p c) -> p n c", p=P, c=PACK))
        nc.scalar.dma_start(out=bias_raw[:], in_=item_bias.rearrange("(n p c) -> p n c", p=P, c=PACK))

        xs_raw = keep.tile([P, U], U8, name="xs_raw", align_bytes=64)
        nc.vector.memset(xs_raw[:].bitcast(I32), 0)
        ident = keep.tile([P, P], F32, name="ident")
        make_identity(nc, ident[:])

        x_flat = x_words.rearrange("g p u t -> p g (u t)")
        x_raw, w_raw = {}, {}

        def load_x(h):
            x_raw[h] = keep.tile([P, PASSES, KP], I32, name="x_raw%d" % h)
            nc.sync.dma_start(out=x_raw[h][:], in_=x_flat[:, :, h * KP * PACK : (h + 1) * KP * PACK].bitcast(I32))

        def load_w(n, g):
            w_raw[n, g] = keep.tile([P, PACK, NT], BF16, name="w_raw%d_%d" % (n, g))
            nc.sync.dma_start(
                out=w_raw[n, g][:],
                in_=w[g * KP : (g + 1) * KP, n * NT : (n + 1) * NT].rearrange("(p t) c -> p t c", t=PACK),
            )

        load_w(0, 0)
        load_x(0)
        for q in range(4):
            nc.sync.dma_start(
                out=xs_raw[32 * q : 32 * q + 4 * PASSES, :].bitcast(I32),
                in_=x_scales[:, 4 * q : 4 * q + 4, :].bitcast(I32),
            )
        load_w(0, 1)
        load_w(0, 2)
        load_x(1)
        for n in range(1, TILES):
            for g in range(PASSES):
                load_w(n, g)

        ncount = HALVES * PACK
        nitem = TILES * PACK
        positives = keep.tile([P, ncount + nitem], F32, name="positives")
        logs = keep.tile([P, ncount + nitem], F32, name="logs")
        inv_count = keep.tile([P, ncount], F32, name="inv_count")
        bias32 = keep.tile([P, nitem], F32, name="bias32")
        x_scale = keep.tile([P, U], U8, name="x_scale", align_bytes=64)
        y_scale = keep.tile([P, N], U8, name="y_scale", align_bytes=64)
        x_codes, w_grouped, w_codes, w_scale, bias_rows = {}, {}, {}, {}, {}
        log_bank, bias_bank, acc, share, y32, y16, y_codes = {}, {}, {}, {}, {}, {}, {}

        def sort_x_codes(h):
            x_codes[h] = keep.tile([P, PACK, PASSES, P], U32, name="x_codes%d" % h, align_bytes=64)
            nc.vector.tensor_copy(
                out=x_codes[h][:].bitcast(I32).rearrange("p t g (b i) -> p g b t i", i=4),
                in_=x_raw[h][:].rearrange("p g (b i t) -> p g b t i", i=4, t=PACK),
            )

        def sort_x_scales():
            nc.vector.tensor_copy(
                out=x_scale[:].rearrange("p (h t b i) -> p h b t i", h=HALVES, t=PACK, i=16),
                in_=xs_raw[:].rearrange("p (h b i t) -> p h b t i", h=HALVES, t=PACK, i=16),
            )

        def interleave(copy, dst, src, lo, hi):
            copy(
                out=dst[:, lo * PACK : hi * PACK].rearrange("p (c i t) -> p c t i", i=4, t=PACK),
                in_=src[:, :, lo:hi].rearrange("p t (c i) -> p c t i", i=4),
            )

        def on_gpsimd(out, in_):
            nc.gpsimd.tensor_scalar(out=out, in0=in_, scalar1=1.0, scalar2=0.0, op0=ALU.mult, op1=ALU.add)

        def group_w(copy, n, g, lo, hi):
            if (n, g) not in w_grouped:
                if n > 0 and g != 1:
                    w_grouped[n, g] = ring.tile([P, NT * PACK], BF16, name="w_grouped_one", bufs=1, align_bytes=64)
                else:
                    w_grouped[n, g] = ring.tile([P, NT * PACK], BF16, name="w_grouped", bufs=3, align_bytes=64)
            if copy is on_gpsimd:
                copy(
                    out=w_grouped[n, g][:, lo * PACK : hi * PACK].rearrange("p (c t) -> p c t", t=PACK),
                    in_=w_raw[n, g][:, :, lo:hi].rearrange("p t c -> p c t"),
                )
            else:
                interleave(copy, w_grouped[n, g], w_raw[n, g], lo, hi)

        def quantize_w(n, g):
            w_codes[n, g] = keep.tile([P, NT], U32, name="w_codes%d_%d" % (n, g), align_bytes=64)
            w_scale[n, g] = keep.tile([P, NT], U8, name="w_scale%d_%d" % (n, g), align_bytes=64)
            nc.vector.quantize_mx(out=w_codes[n, g][:].bitcast(FP8X4), scales=w_scale[n, g][:], in_=w_grouped[n, g][:])

        def spread(bank, cols, first):
            by_slot = bank[:].rearrange("q (p c) -> q c p", c=PACK)
            for c in range(PACK):
                col = first + c
                nc.tensor.transpose(by_slot[:, c, :], cols[:, col : col + 1].to_broadcast([P, P]), ident[:])

        def spread_items(n):
            log_bank[n] = psum.tile([P, NT], F32, name="log_bank", bufs=2)
            spread(log_bank[n], logs, ncount + n * PACK)
            bias_bank[n] = psum.tile([P, NT], F32, name="bias_bank", bufs=2)
            spread(bias_bank[n], bias32, n * PACK)

        def mx_pass(i, t, g):
            n, h = divmod(i, HALVES)
            if g == 0:
                acc[i, t] = psum.tile([P, NT], F32, name="acc", bufs=4)
            lo = h * KP + t * P
            nc.tensor.matmul_mx(
                out=acc[i, t][:],
                lhsT=x_codes[h][:, t, g, :].bitcast(FP8X4),
                lhsT_scale=x_scale[4 * g : P, lo : lo + P],
                rhs=w_codes[n, g][:].bitcast(FP8X4),
                rhs_scale=w_scale[n, g][:],
                start=(g == 0),
                stop=(g == PASSES - 1),
            )


        def sigmoid(i, t):
            n, h = divmod(i, HALVES)
            col = h * PACK + t
            share[i, t] = ring.tile([P, NT], F32, name="share", bufs=8)
            nc.scalar.activation(
                out=share[i, t][:], in_=log_bank[n][:], func=ACT.Sigmoid, bias=logs[:, col : col + 1], scale=-1.0
            )

        def divide(i, t, lo, hi):
            h = i % HALVES
            col = h * PACK + t
            if i not in y32:
                y32[i] = keep.tile([P, PACK, NT], F32, name="y32_%d" % i)
            nc.vector.scalar_tensor_tensor(
                out=y32[i][:, t, lo:hi], in0=share[i, t][:, lo:hi], scalar=inv_count[:, col : col + 1],
                in1=acc[i, t][:, lo:hi],
                op0=ALU.mult, op1=ALU.mult,
            )

        def add_bias(i, lo, hi):
            n = i // HALVES
            nc.vector.tensor_tensor(
                out=y32[i][:, :, lo:hi], in0=y32[i][:, :, lo:hi],
                in1=bias_bank[n][:, lo:hi].unsqueeze(1).to_broadcast([P, PACK, hi - lo]), op=ALU.add,
            )

        def copy_bias(copy, n):
            bias_rows[n] = keep.tile([P, HALF], F32, name="bias_rows%d" % n)
            copy(out=bias_rows[n][:], in_=bias_bank[n][:, HALF:])

        def add_bias_gpsimd(i):
            nc.gpsimd.tensor_tensor(
                out=y32[i][:, :, HALF:], in0=y32[i][:, :, HALF:],
                in1=bias_rows[i // HALVES][:].unsqueeze(1).to_broadcast([P, PACK, HALF]), op=ALU.add,
            )

        def store_scales(lo, hi):
            for q in range(4):
                queue = nc.sync if q % 2 == 0 or lo == 0 else nc.scalar
                queue.dma_start(
                    out=out_2[:, 4 * q : 4 * q + 4, lo:hi].bitcast(I32),
                    in_=y_scale[32 * q : 32 * q + 4 * HALVES, lo:hi].bitcast(I32),
                )

        def store_y(i, lo, hi):
            n, h = divmod(i, HALVES)
            rows = out_0[h * KP : (h + 1) * KP, n * NT + lo : n * NT + hi].rearrange("(p t) m -> p t m", t=PACK)
            nc.sync.dma_start(out=rows, in_=y32[i][:, :, lo:hi])

        def group_y(copy, i, lo, hi):
            if i not in y16:
                y16[i] = ring.tile([P, NT * PACK], BF16, name="y16", bufs=3, align_bytes=64)
            interleave(copy, y16[i], y32[i], lo, hi)

        def quantize_y(i, lo, hi):
            n, h = divmod(i, HALVES)
            if i not in y_codes:
                y_codes[i] = keep.tile([P, NT], U32, name="y_codes%d" % i, align_bytes=64)
            nc.vector.quantize_mx(
                out=y_codes[i][:, lo:hi].bitcast(FP8X4),
                scales=y_scale[4 * h : P, n * NT + lo : n * NT + hi],
                in_=y16[i][:, lo * PACK : hi * PACK],
            )

        def store_codes(i, lo, hi):
            n, h = divmod(i, HALVES)
            dst = out_1[h].rearrange("p m t -> p (m t)")[:, (n * NT + lo) * PACK : (n * NT + hi) * PACK]
            nc.sync.dma_start(out=dst.bitcast(I32), in_=y_codes[i][:, lo:hi].bitcast(I32))

        on_vector, on_scalar = nc.vector.tensor_copy, nc.scalar.copy

        nc.vector.tensor_scalar(
            out=positives[:, :ncount], in0=count_raw[:].rearrange("p h t -> p (h t)"),
            scalar1=COUNT_FLOOR, scalar2=None, op0=ALU.max,
        )
        nc.vector.tensor_copy(out=positives[:, ncount:], in_=shrink_raw[:].rearrange("p n c -> p (n c)"))
        nc.vector.tensor_copy(out=bias32[:], in_=bias_raw[:].rearrange("p n c -> p (n c)"))
        nc.vector.reciprocal(out=inv_count[:], in_=positives[:, :ncount])
        nc.scalar.activation(out=logs[:], in_=positives[:], func=ACT.Ln)
        spread_items(0)
        sigmoid(0, 0)
        group_w(on_vector, 0, 0, 0, NT)
        sort_x_codes(0)
        quantize_w(0, 0)
        for g in (1, 2):
            group_w(on_vector, 0, g, 0, HEAD_V_COLS)
            group_w(on_scalar, 0, g, HEAD_V_COLS, NT)
        sort_x_scales()
        quantize_w(0, 1)
        quantize_w(0, 2)
        for t in range(PACK):
            mx_pass(0, t, 0)
        for t in range(PACK):
            mx_pass(0, t, 1)
            mx_pass(0, t, 2)
        for t in range(1, PACK):
            sigmoid(0, t)
        sort_x_codes(1)

        last = STEPS - 1
        for i in range(last):
            n, h = divmod(i, HALVES)
            more = n + 1 < TILES
            if i > 1:
                quantize_y(i - 2, 0, NT)
                store_codes(i - 2, 0, NT)
            if i - 2 == STEPS // 2 - 1:
                store_scales(0, N // 2)
            if h == 0 and i > 0:
                quantize_w(n, 1)
                quantize_w(n, 2)
                for t in range(PACK):
                    mx_pass(i, t, 1)
                    mx_pass(i, t, 2)
            if i == 1:
                add_bias(0, 0, HALF)
            if h == 1 and more:
                quantize_w(n + 1, 0)
            if more:
                group_w(on_gpsimd, n + 1, 2 * h, 0, NT)
            if h == 1 and more:
                group_w(on_scalar, n + 1, 1, 0, NT)
            if i == last - 1:
                copy_bias(on_vector, n - 1)
            if h == 0:
                for t in range(PACK):
                    sigmoid(i + 1, t)
            if i == last - 1:
                copy_bias(on_scalar, n)
            if i > 0:
                for lo in (0, HALF):
                    if lo == HALF and not more:
                        add_bias_gpsimd(i - 1)
                    elif (i, lo) != (1, 0):
                        add_bias(i - 1, lo, lo + HALF)
                    group_y(on_scalar, i - 1, lo, lo + HALF)
                store_y(i - 1, 0, NT)
            if h == 0 and more:
                spread_items(n + 1)
            if h == 1 and more:
                for t in range(PACK):
                    sigmoid(i + 1, t)
            for t in range(PACK):
                divide(i, t, 0, NT)
                for g in range(PASSES if h == 0 else 1):
                    mx_pass(i + 1, t, g)

        cut = HALF + QUARTER
        divide(last, 0, 0, HALF)
        add_bias_gpsimd(last - 1)
        add_bias(last - 1, 0, HALF)
        for lo in (0, HALF):
            store_y(last - 1, lo, lo + HALF)
            group_y(on_scalar, last - 1, lo, lo + HALF)
        for t in range(1, PACK):
            divide(last, t, 0, HALF)
        divide(last, 0, HALF, NT)
        add_bias(last, 0, HALF)
        store_y(last, 0, HALF)
        group_y(on_scalar, last, 0, HALF)
        quantize_y(last - 2, 0, NT)
        store_codes(last - 2, 0, NT)
        for t in range(1, PACK):
            divide(last, t, HALF, NT)
        quantize_y(last - 1, 0, NT)
        store_codes(last - 1, 0, NT)
        add_bias(last, HALF, cut)
        store_y(last, HALF, cut)
        group_y(on_scalar, last, HALF, cut)
        add_bias(last, cut, NT)
        store_y(last, cut, NT)
        quantize_y(last, 0, HALF)
        store_codes(last, 0, HALF)
        group_y(on_vector, last, cut, NT)
        quantize_y(last, HALF, cut)
        quantize_y(last, cut, NT)
        store_codes(last, HALF, NT)
        store_scales(N // 2, N)
